import numpy as np
import ml_dtypes


def mxq(x, axis, fmt="e4m3"):
    dtype, down = {"e4m3": (ml_dtypes.float8_e4m3fn, 7), "e5m2": (ml_dtypes.float8_e5m2, 14)}[fmt]
    v = np.moveaxis(np.asarray(x, np.float32).astype(ml_dtypes.bfloat16).astype(np.float64), axis, -1)
    blocks = v.reshape(v.shape[:-1] + (-1, 32))
    amax = np.abs(blocks).max(-1, keepdims=True)
    byte = np.maximum(np.where(amax > 0, np.frexp(amax)[1] - 1 + 127, 0) - down, 1)
    scale = np.exp2(byte - 127.0)
    codes = (blocks / scale).astype(np.float32).astype(dtype).astype(np.float64)
    return np.moveaxis((codes * scale).reshape(v.shape), -1, axis)


WIDE = False


def mx_kscale(k):
    if not WIDE:
        return np.ones(k)
    levels = np.array([30, -30])
    if k % 512:
        return np.exp2(np.random.permutation(np.resize(levels, k // 32))).repeat(32)
    a = np.empty((k // 512, 16))
    for p in range(k // 512):
        a[p, :8] = np.random.permutation(np.resize(levels, 8))
        for g in range(8):
            far = levels[np.abs(levels - a[p, g]) >= 10]
            a[p, g + 8] = far[np.random.randint(len(far))]
    return np.exp2(a.ravel()).repeat(32)


def f64(x):
    return np.asarray(x).astype(np.float64)


def striped(idx):
    return np.tile(np.asarray(idx).reshape(-1, 16).T, (8, 1)).astype(np.uint16)


def unstriped(offs):
    return offs[:16].T.reshape(-1).astype(np.int64)


E2M1 = np.array([0.0, 0.5, 1.0, 1.5, 2.0, 3.0, 4.0, 6.0, -0.0, -0.5, -1.0, -1.5, -2.0, -3.0, -4.0, -6.0])


def pack_weight(w, fmt):
    k, n = w.shape
    w = f64(np.asarray(w, np.float32).astype(ml_dtypes.bfloat16)).reshape(k // 32, 32, n)
    amax = np.abs(w).max(1)
    if fmt in ("e4m3", "e5m2"):
        byte = np.frexp(amax)[1] - 1 + 127 - (7 if fmt == "e4m3" else 14)
    else:
        mant, ex = np.frexp(amax / 6.0)
        byte = np.where(mant > 0.5, ex, ex - 1) + 127
    byte = np.clip(np.where(amax > 0, byte, 1), 1, 254)
    scaled = (w * np.exp2(127.0 - byte)[:, None, :]).reshape(k, n).astype(np.float32)
    by_word = np.ascontiguousarray(scaled.reshape(k // 512, 128, 4, n).transpose(0, 1, 3, 2))
    if fmt in ("e4m3", "e5m2"):
        words = by_word.astype(ml_dtypes.float8_e4m3fn if fmt == "e4m3" else ml_dtypes.float8_e5m2).view(np.uint8)
    else:
        c = by_word.astype(ml_dtypes.float4_e2m1fn).view(np.uint8) & 0xF
        words = (c[..., 0::2] | (c[..., 1::2] << 4)).reshape(k // 512, 128, 2 * n)
    return np.ascontiguousarray(words), np.ascontiguousarray(byte.astype(np.uint8).reshape(k // 512, 16, n))


def unpack_weight(words, scales, fmt):
    g, _, n = scales.shape
    words = np.ascontiguousarray(words).reshape(g, 128, n, -1)
    if fmt in ("e4m3", "e5m2"):
        vals = words.view(ml_dtypes.float8_e4m3fn if fmt == "e4m3" else ml_dtypes.float8_e5m2).astype(np.float64)
    else:
        nib = np.empty((g, 128, n, 4), np.uint8)
        nib[..., 0::2] = words & 0xF
        nib[..., 1::2] = words >> 4
        vals = E2M1[nib]
    vals = vals * np.repeat(np.exp2(scales.astype(np.float64) - 127.0), 8, axis=1)[..., None]
    return vals.transpose(0, 1, 3, 2).reshape(g * 512, n)


def e4m3fn_bytes(y):
    return np.clip(np.asarray(y, np.float64), -448.0, 448.0).astype(np.float32).astype(ml_dtypes.float8_e4m3fn).view(np.uint8)


def e4m3fn_values(b):
    return np.asarray(b, np.uint8).view(ml_dtypes.float8_e4m3fn).astype(np.float64)


K, T, J, R, F, Z, V, N = 512, 1024, 256, 512, 512, 1024, 1024, 256


def setup_inputs():
    n = np.random.standard_normal
    idx = np.random.permutation(T)[:J]
    idx2 = np.random.permutation(Z)[:J]
    idx3 = np.random.permutation(V)[:J]
    idx4 = np.random.permutation(V)[:J]
    fk = mx_kscale(K)
    ff = mx_kscale(F)
    fr = mx_kscale(R)
    xtp = pack_weight(n((K, T)) / fk[:, None], "e5m2")
    xop = pack_weight(n((F, Z)) / ff[:, None], "e4m3")
    wp = pack_weight(n((K, R)) * 1 / np.sqrt(K) * fk[:, None], "e2m1")
    w0p = pack_weight(n((F, R)) * 1 / np.sqrt(F) * ff[:, None], "e2m1")
    wbp = pack_weight(n((R, N)) * 1 / np.sqrt(R) / fr[:, None], "e2m1")
    return {
        "xt_words": xtp[0],
        "xt_scales": xtp[1],
        "xo_words": xop[0],
        "xo_scales": xop[1],
        "w_words": wp[0],
        "w_scales": wp[1],
        "w0_words": w0p[0],
        "w0_scales": w0p[1],
        "ca": e4m3fn_bytes(60.0 * n((R, V))),
        "st": (np.random.uniform(0.004, 0.012, (R, 1)) * fr[:, None]).astype(np.float32),
        "wb_words": wbp[0],
        "wb_scales": wbp[1],
        "offs": striped(idx),
        "offs2": striped(idx2),
        "offs3": striped(idx3),
        "offs4": striped(idx4),
    }


def reference(xt_words, xt_scales, xo_words, xo_scales, w_words, w_scales, w0_words, w0_scales, ca, st, wb_words, wb_scales, offs, offs2, offs3, offs4):
    idx = unstriped(offs)
    idx2 = unstriped(offs2)
    idx3 = unstriped(offs3)
    idx4 = unstriped(offs4)
    xtu = unpack_weight(xt_words, xt_scales, "e5m2")
    xou = unpack_weight(xo_words, xo_scales, "e4m3")
    wu = unpack_weight(w_words, w_scales, "e2m1")
    w0u = unpack_weight(w0_words, w0_scales, "e2m1")
    wbu = unpack_weight(wb_words, wb_scales, "e2m1")
    xtidxg = xtu[:, idx]
    xoidx2g = xou[:, idx2]
    a = wu.T @ xtidxg + w0u.T @ xoidx2g
    g1 = (e4m3fn_values(ca)[:, idx3] - e4m3fn_values(ca)[:, idx4]) * f64(st)
    hid = a * g1
    hidq = mxq(hid, 0, "e4m3")
    p = wbu.T @ hidq
    return p

@@ -1,0 +1,161 @@
+from contextlib import ExitStack
+
+import concourse.mybir as mybir
+from concourse.masks import make_identity
+
+T, J, R, N = 1024, 256, 512, 256
+FLOPS = 335544320
+
+P = 128
+PACK = 4
+HALVES = J // P
+
+F32 = mybir.dt.float32
+BF16 = mybir.dt.bfloat16
+I32 = mybir.dt.int32
+U32 = mybir.dt.uint32
+U16 = mybir.dt.uint16
+U8 = mybir.dt.uint8
+FP8 = mybir.dt.float8_e4m3fn
+E4M3X4 = mybir.dt.float8_e4m3fn_x4
+E5M2X4 = mybir.dt.float8_e5m2_x4
+E2M1X4 = mybir.dt.float4_e2m1fn_x4
+COPY = mybir.ActivationFunctionType.Copy
+MULT = mybir.AluOpType.mult
+
+
+def tile_list_entrydiff_kernel(tc, xt_words, xt_scales, xo_words, xo_scales, w_words, w_scales,
+                                    w0_words, w0_scales, ca, st, wb_words, wb_scales,
+                                    offs, offs2, offs3, offs4, out):
+    nc = tc.nc
+    with ExitStack() as ctx:
+        sb = ctx.enter_context(tc.tile_pool(name="sb", bufs=1))
+        ps = ctx.enter_context(tc.psum_pool(name="ps", bufs=1))
+
+        def new(name, width, dtype):
+            return sb.tile([P, width], dtype, name=name, align_bytes=64)
+
+        def load_list(name, src):
+            tile = sb.tile([P, J // 16], U16, name=name)
+            nc.sync.dma_start(tile[:], src)
+            return tile
+
+        def zeroed_plane(name, width):
+            tile = new(name, width, U8)
+            nc.vector.memset(tile[:].bitcast(I32), 0)
+            return tile
+
+        def load_scales(plane, src):
+            rows = src[0].bitcast(I32)
+            for q in range(4):
+                nc.sync.dma_start(plane[32 * q:32 * q + 4, :].bitcast(I32), rows[4 * q:4 * q + 4, :])
+
+        xt_plane = zeroed_plane("xt_plane", T)
+        xo_plane = zeroed_plane("xo_plane", T)
+        w_plane = zeroed_plane("w_plane", R)
+        w0_plane = zeroed_plane("w0_plane", R)
+        wb_plane = zeroed_plane("wb_plane", N)
+
+        ident = new("ident", P, F32)
+        make_identity(nc, ident[:])
+
+        ca_rows = ca.rearrange("(p t) v -> t p v", t=PACK)
+        store = [new("store%d" % t, T, U8) for t in range(PACK)]
+        nc.sync.dma_start(store[0][:], ca_rows[0])
+        list3 = load_list("list3", offs3)
+        list4 = load_list("list4", offs4)
+        step = new("step", PACK, F32)
+        nc.scalar.dma_start(step[:], st.rearrange("(p t) o -> p (t o)", t=PACK))
+        for t in range(1, PACK):
+            nc.sync.dma_start(store[t][:], ca_rows[t])
+        xt_sb = new("xt_sb", T, I32)
+        nc.sync.dma_start(xt_sb[:], xt_words[0].rearrange("p c r -> p (c r)").bitcast(I32))
+        list1 = load_list("list1", offs)
+        xo_sb = new("xo_sb", T, I32)
+        nc.sync.dma_start(xo_sb[:], xo_words[0].rearrange("p c r -> p (c r)").bitcast(I32))
+        list2 = load_list("list2", offs2)
+        w_sb = new("w_sb", 2 * R, U8)
+        nc.sync.dma_start(w_sb[:].bitcast(I32), w_words[0].bitcast(I32))
+        w0_sb = new("w0_sb", 2 * R, U8)
+        nc.sync.dma_start(w0_sb[:].bitcast(I32), w0_words[0].bitcast(I32))
+        load_scales(xt_plane, xt_scales)
+        load_scales(xo_plane, xo_scales)
+        load_scales(w_plane, w_scales)
+        load_scales(w0_plane, w0_scales)
+        wb_sb = new("wb_sb", 2 * N, U8)
+        nc.sync.dma_start(wb_sb[:].bitcast(I32), wb_words[0].bitcast(I32))
+        load_scales(wb_plane, wb_scales)
+
+        neg_step = new("neg_step", PACK, F32)
+        nc.scalar.activation(neg_step[:], step[:], COPY, scale=-1.0)
+
+        g_ps = [ps.tile([P, R], F32, name="g_ps%d" % h, tag="g_ps%d" % h) for h in range(HALVES)]
+        for t in range(PACK):
+            for side, (lst, factor) in enumerate(((list3, step), (list4, neg_step))):
+                codes = new("codes%d_%d" % (t, side), J, U8)
+                nc.vector.tensor_copy(codes[:], store[t][:].indirect(lst[:]))
+                vals = new("vals%d_%d" % (t, side), J, F32)
+                nc.scalar.activation(vals[:], codes[:].bitcast(FP8), COPY, scale=factor[:, t:t + 1])
+                for h in range(HALVES):
+                    nc.tensor.matmul(g_ps[h][:, t * P:(t + 1) * P], lhsT=vals[:, h * P:(h + 1) * P], rhs=ident[:],
+                                     is_transpose=True, start=(side == 0), stop=(side == 1))
+        g_sb = []
+        for h in range(HALVES):
+            g = new("g_sb%d" % h, R, F32)
+            nc.scalar.copy(g[:].rearrange("j (u p e) -> j u p e", u=2, e=2),
+                           g_ps[h][:].rearrange("j (u e p) -> j u p e", u=2, e=2))
+            g_sb.append(g)
+
+        xt_g = new("xt_g", J, U32)
+        nc.vector.tensor_copy(xt_g[:], xt_sb[:].bitcast(U32).indirect(list1[:]))
+        xt_gs = new("xt_gs", J, U8)
+        nc.vector.tensor_copy(xt_gs[:], xt_plane[:].indirect(list1[:]))
+        a_ps = [ps.tile([P, R], F32, name="a_ps%d" % h) for h in range(HALVES)]
+        for h in range(HALVES):
+            cols = slice(h * P, (h + 1) * P)
+            nc.tensor.matmul_mx(a_ps[h][:], lhsT=xt_g[:, cols].bitcast(E5M2X4), lhsT_scale=xt_gs[:, cols],
+                                rhs=w_sb[:].bitcast(E2M1X4), rhs_scale=w_plane[:], start=True, stop=False)
+        for h in range(HALVES):
+            part = list2[:, h * 8:(h + 1) * 8]
+            xo_g = new("xo_g%d" % h, P, U32)
+            nc.vector.tensor_copy(xo_g[:], xo_sb[:].bitcast(U32).indirect(part))
+            xo_gs = new("xo_gs%d" % h, P, U8)
+            nc.vector.tensor_copy(xo_gs[:], xo_plane[:].indirect(part))
+            nc.tensor.matmul_mx(a_ps[h][:], lhsT=xo_g[:].bitcast(E4M3X4), lhsT_scale=xo_gs[:],
+                                rhs=w0_sb[:].bitcast(E2M1X4), rhs_scale=w0_plane[:], start=False, stop=True)
+
+        grouped = []
+        for h in range(HALVES):
+            turned = ps.tile([P, 2 * P], F32, name="turned%d" % h)
+            for u in range(2):
+                hid_t = new("hid_t%d_%d" % (h, u), R // 2, BF16)
+                nc.vector.tensor_tensor(hid_t[:].rearrange("j (p e) -> j p e", e=2),
+                                        a_ps[h][:].rearrange("j (p u e) -> j u p e", u=2, e=2)[:, u],
+                                        g_sb[h][:].rearrange("j (u p e) -> j u p e", u=2, e=2)[:, u], MULT)
+                nc.tensor.transpose(turned[:, u * P:(u + 1) * P], hid_t[:].bitcast(F32), ident[:])
+            hid = new("hid%d" % h, R, BF16)
+            nc.scalar.copy(hid[:].bitcast(F32).rearrange("p (j u) -> p j u", u=2),
+                           turned[:].rearrange("p (u j) -> p j u", u=2))
+            grouped.append(hid)
+
+        for h in range(HALVES):
+            hid_q = new("hid_q%d" % h, P, U32)
+            hid_s = new("hid_s%d" % h, P, U8)
+            nc.vector.quantize_mx(hid_q[:].bitcast(E4M3X4), hid_s[:], grouped[h][:])
+            for b in range(N // P):
+                o_ps = ps.tile([P, P], F32, name="o_ps%d_%d" % (h, b), tag=("o_ps%d" if h == 0 else "g_ps%d") % b)
+                nc.tensor.matmul_mx(o_ps[:],
+                                    lhsT=wb_sb[:, 2 * b * P:2 * (b + 1) * P].bitcast(E2M1X4),
+                                    lhsT_scale=wb_plane[:, b * P:(b + 1) * P],
+                                    rhs=hid_q[:].bitcast(E4M3X4), rhs_scale=hid_s[:], start=True, stop=True)
+                o_sb = new("o_sb%d_%d" % (h, b), P, F32)
+                dst = out[b * P:(b + 1) * P, h * P:(h + 1) * P]
+                if h == 1 and b == 0:
+                    nc.vector.tensor_copy(o_sb[:], o_ps[:])
+                    nc.sync.dma_start(dst, o_sb[:])
+                elif h == 1:
+                    nc.scalar.copy(o_sb[:], o_ps[:])
+                    nc.scalar.dma_start(dst, o_sb[:])
+                else:
+                    nc.scalar.copy(o_sb[:], o_ps[:])
+                    nc.sync.dma_start(dst, o_sb[:])

@@ -66,21 +66,22 @@ def tile_list_entrydiff_kernel(tc, xt_words, xt_scales, xo_words, xo_scales, w_w
         list4 = load_list("list4", offs4)
         step = new("step", PACK, F32)
         nc.scalar.dma_start(step[:], st.rearrange("(p t) o -> p (t o)", t=PACK))
-        for t in range(1, PACK):
+        for t in (1, 2):
             nc.sync.dma_start(store[t][:], ca_rows[t])
         xt_sb = new("xt_sb", T, I32)
         nc.sync.dma_start(xt_sb[:], xt_words[0].rearrange("p c r -> p (c r)").bitcast(I32))
         list1 = load_list("list1", offs)
+        load_scales(xt_plane, xt_scales)
+        w_sb = new("w_sb", 2 * R, U8)
+        nc.sync.dma_start(w_sb[:].bitcast(I32), w_words[0].bitcast(I32))
+        load_scales(w_plane, w_scales)
+        nc.sync.dma_start(store[3][:], ca_rows[3])
         xo_sb = new("xo_sb", T, I32)
         nc.sync.dma_start(xo_sb[:], xo_words[0].rearrange("p c r -> p (c r)").bitcast(I32))
         list2 = load_list("list2", offs2)
-        w_sb = new("w_sb", 2 * R, U8)
-        nc.sync.dma_start(w_sb[:].bitcast(I32), w_words[0].bitcast(I32))
+        load_scales(xo_plane, xo_scales)
         w0_sb = new("w0_sb", 2 * R, U8)
         nc.sync.dma_start(w0_sb[:].bitcast(I32), w0_words[0].bitcast(I32))
-        load_scales(xt_plane, xt_scales)
-        load_scales(xo_plane, xo_scales)
-        load_scales(w_plane, w_scales)
         load_scales(w0_plane, w0_scales)
         wb_sb = new("wb_sb", 2 * N, U8)
         nc.sync.dma_start(wb_sb[:].bitcast(I32), wb_words[0].bitcast(I32))
@@ -89,50 +90,68 @@ def tile_list_entrydiff_kernel(tc, xt_words, xt_scales, xo_words, xo_scales, w_w
         neg_step = new("neg_step", PACK, F32)
         nc.scalar.activation(neg_step[:], step[:], COPY, scale=-1.0)
 
-        g_ps = [ps.tile([P, R], F32, name="g_ps%d" % h, tag="g_ps%d" % h) for h in range(HALVES)]
-        for t in range(PACK):
+        g_ps = {(h, u): ps.tile([P, 2 * P], F32, name="g_ps%d_%d" % (h, u), tag="bank%d" % (2 * u + h))
+                for h in range(HALVES) for u in range(2)}
+        g_sb = {}
+
+        def difference(t):
+            u, e = divmod(t, 2)
             for side, (lst, factor) in enumerate(((list3, step), (list4, neg_step))):
                 codes = new("codes%d_%d" % (t, side), J, U8)
                 nc.vector.tensor_copy(codes[:], store[t][:].indirect(lst[:]))
                 vals = new("vals%d_%d" % (t, side), J, F32)
                 nc.scalar.activation(vals[:], codes[:].bitcast(FP8), COPY, scale=factor[:, t:t + 1])
                 for h in range(HALVES):
-                    nc.tensor.matmul(g_ps[h][:, t * P:(t + 1) * P], lhsT=vals[:, h * P:(h + 1) * P], rhs=ident[:],
+                    nc.tensor.matmul(g_ps[h, u][:, e * P:(e + 1) * P], lhsT=vals[:, h * P:(h + 1) * P], rhs=ident[:],
                                      is_transpose=True, start=(side == 0), stop=(side == 1))
-        g_sb = []
-        for h in range(HALVES):
-            g = new("g_sb%d" % h, R, F32)
-            nc.scalar.copy(g[:].rearrange("j (u p e) -> j u p e", u=2, e=2),
-                           g_ps[h][:].rearrange("j (u e p) -> j u p e", u=2, e=2))
-            g_sb.append(g)
+            if e == 1:
+                for h in range(HALVES):
+                    g = new("g_sb%d_%d" % (h, u), 2 * P, F32)
+                    nc.scalar.copy(g[:].rearrange("j (p e) -> j p e", e=2),
+                                   g_ps[h, u][:].rearrange("j (e p) -> j p e", e=2))
+                    g_sb[h, u] = g
 
+        pieces = [(0, 0, R), (1, 0, R // 2), (1, R // 2, R)]
+        a_ps = [ps.tile([P, hi - lo], F32, name="a_ps%d" % i, tag="bank%d" % (4 + i))
+                for i, (h, lo, hi) in enumerate(pieces)]
+
+        for t in range(3):
+            difference(t)
         xt_g = new("xt_g", J, U32)
         nc.vector.tensor_copy(xt_g[:], xt_sb[:].bitcast(U32).indirect(list1[:]))
         xt_gs = new("xt_gs", J, U8)
         nc.vector.tensor_copy(xt_gs[:], xt_plane[:].indirect(list1[:]))
-        a_ps = [ps.tile([P, R], F32, name="a_ps%d" % h) for h in range(HALVES)]
-        for h in range(HALVES):
+        for i, (h, lo, hi) in enumerate(pieces):
             cols = slice(h * P, (h + 1) * P)
-            nc.tensor.matmul_mx(a_ps[h][:], lhsT=xt_g[:, cols].bitcast(E5M2X4), lhsT_scale=xt_gs[:, cols],
-                                rhs=w_sb[:].bitcast(E2M1X4), rhs_scale=w_plane[:], start=True, stop=False)
+            nc.tensor.matmul_mx(a_ps[i][:], lhsT=xt_g[:, cols].bitcast(E5M2X4), lhsT_scale=xt_gs[:, cols],
+                                rhs=w_sb[:, 2 * lo:2 * hi].bitcast(E2M1X4), rhs_scale=w_plane[:, lo:hi],
+                                start=True, stop=False)
+        difference(3)
         for h in range(HALVES):
             part = list2[:, h * 8:(h + 1) * 8]
             xo_g = new("xo_g%d" % h, P, U32)
             nc.vector.tensor_copy(xo_g[:], xo_sb[:].bitcast(U32).indirect(part))
             xo_gs = new("xo_gs%d" % h, P, U8)
             nc.vector.tensor_copy(xo_gs[:], xo_plane[:].indirect(part))
-            nc.tensor.matmul_mx(a_ps[h][:], lhsT=xo_g[:].bitcast(E4M3X4), lhsT_scale=xo_gs[:],
-                                rhs=w0_sb[:].bitcast(E2M1X4), rhs_scale=w0_plane[:], start=False, stop=True)
+            for i, (half, lo, hi) in enumerate(pieces):
+                if half == h:
+                    nc.tensor.matmul_mx(a_ps[i][:], lhsT=xo_g[:].bitcast(E4M3X4), lhsT_scale=xo_gs[:],
+                                        rhs=w0_sb[:, 2 * lo:2 * hi].bitcast(E2M1X4), rhs_scale=w0_plane[:, lo:hi],
+                                        start=False, stop=True)
 
         grouped = []
         for h in range(HALVES):
-            turned = ps.tile([P, 2 * P], F32, name="turned%d" % h)
+            turned = ps.tile([P, 2 * P], F32, name="turned%d" % h, tag="bank%d" % h)
+            hid_t = [new("hid_t%d_%d" % (h, u), R // 2, BF16) for u in range(2)]
+            for i, (half, lo, hi) in enumerate(pieces):
+                if half == h:
+                    for u in range(2):
+                        cols = slice(lo // 2, hi // 2)
+                        nc.vector.tensor_tensor(hid_t[u][:, cols].rearrange("j (p e) -> j p e", e=2),
+                                                a_ps[i][:].rearrange("j (p u e) -> j u p e", u=2, e=2)[:, u],
+                                                g_sb[h, u][:, cols].rearrange("j (p e) -> j p e", e=2), MULT)
             for u in range(2):
-                hid_t = new("hid_t%d_%d" % (h, u), R // 2, BF16)
-                nc.vector.tensor_tensor(hid_t[:].rearrange("j (p e) -> j p e", e=2),
-                                        a_ps[h][:].rearrange("j (p u e) -> j u p e", u=2, e=2)[:, u],
-                                        g_sb[h][:].rearrange("j (u p e) -> j u p e", u=2, e=2)[:, u], MULT)
-                nc.tensor.transpose(turned[:, u * P:(u + 1) * P], hid_t[:].bitcast(F32), ident[:])
+                nc.tensor.transpose(turned[:, u * P:(u + 1) * P], hid_t[u][:].bitcast(F32), ident[:])
             hid = new("hid%d" % h, R, BF16)
             nc.scalar.copy(hid[:].bitcast(F32).rearrange("p (j u) -> p j u", u=2),
                            turned[:].rearrange("p (u j) -> p j u", u=2))
@@ -143,19 +162,16 @@ def tile_list_entrydiff_kernel(tc, xt_words, xt_scales, xo_words, xo_scales, w_w
             hid_s = new("hid_s%d" % h, P, U8)
             nc.vector.quantize_mx(hid_q[:].bitcast(E4M3X4), hid_s[:], grouped[h][:])
             for b in range(N // P):
-                o_ps = ps.tile([P, P], F32, name="o_ps%d_%d" % (h, b), tag=("o_ps%d" if h == 0 else "g_ps%d") % b)
+                o_ps = ps.tile([P, P], F32, name="o_ps%d_%d" % (h, b), tag="bank%d" % (2, 3, 7, 4)[2 * h + b])
                 nc.tensor.matmul_mx(o_ps[:],
                                     lhsT=wb_sb[:, 2 * b * P:2 * (b + 1) * P].bitcast(E2M1X4),
                                     lhsT_scale=wb_plane[:, b * P:(b + 1) * P],
                                     rhs=hid_q[:].bitcast(E4M3X4), rhs_scale=hid_s[:], start=True, stop=True)
                 o_sb = new("o_sb%d_%d" % (h, b), P, F32)
                 dst = out[b * P:(b + 1) * P, h * P:(h + 1) * P]
-                if h == 1 and b == 0:
+                if b == 0:
                     nc.vector.tensor_copy(o_sb[:], o_ps[:])
-                    nc.sync.dma_start(dst, o_sb[:])
-                elif h == 1:
-                    nc.scalar.copy(o_sb[:], o_ps[:])
-                    nc.scalar.dma_start(dst, o_sb[:])
                 else:
                     nc.scalar.copy(o_sb[:], o_ps[:])
-                    nc.sync.dma_start(dst, o_sb[:])
+                queue = nc.scalar if h == 1 and b == 1 else nc.sync
+                queue.dma_start(dst, o_sb[:])

from contextlib import ExitStack

import concourse.mybir as mybir
from concourse.masks import make_identity

T, J, R, N = 1024, 256, 512, 256
FLOPS = 335544320

P = 128
PACK = 4
HALVES = J // P

F32 = mybir.dt.float32
BF16 = mybir.dt.bfloat16
I32 = mybir.dt.int32
U32 = mybir.dt.uint32
U16 = mybir.dt.uint16
U8 = mybir.dt.uint8
FP8 = mybir.dt.float8_e4m3fn
E4M3X4 = mybir.dt.float8_e4m3fn_x4
E5M2X4 = mybir.dt.float8_e5m2_x4
E2M1X4 = mybir.dt.float4_e2m1fn_x4
COPY = mybir.ActivationFunctionType.Copy
MULT = mybir.AluOpType.mult


def tile_list_entrydiff_kernel(tc, xt_words, xt_scales, xo_words, xo_scales, w_words, w_scales,
                                    w0_words, w0_scales, ca, st, wb_words, wb_scales,
                                    offs, offs2, offs3, offs4, out):
    nc = tc.nc
    with ExitStack() as ctx:
        sb = ctx.enter_context(tc.tile_pool(name="sb", bufs=1))
        ps = ctx.enter_context(tc.psum_pool(name="ps", bufs=1))

        def new(name, width, dtype):
            return sb.tile([P, width], dtype, name=name, align_bytes=64)

        def load_list(name, src):
            tile = sb.tile([P, J // 16], U16, name=name)
            nc.sync.dma_start(tile[:], src)
            return tile

        def zeroed_plane(name, width):
            tile = new(name, width, U8)
            nc.vector.memset(tile[:].bitcast(I32), 0)
            return tile

        def load_scales(plane, src):
            rows = src[0].bitcast(I32)
            for q in range(4):
                nc.sync.dma_start(plane[32 * q:32 * q + 4, :].bitcast(I32), rows[4 * q:4 * q + 4, :])

        xt_plane = zeroed_plane("xt_plane", T)
        xo_plane = zeroed_plane("xo_plane", T)
        w_plane = zeroed_plane("w_plane", R)
        w0_plane = zeroed_plane("w0_plane", R)
        wb_plane = zeroed_plane("wb_plane", N)

        ident = new("ident", P, F32)
        make_identity(nc, ident[:])

        ca_rows = ca.rearrange("(p t) v -> t p v", t=PACK)
        store = [new("store%d" % t, T, U8) for t in range(PACK)]
        nc.sync.dma_start(store[0][:], ca_rows[0])
        list3 = load_list("list3", offs3)
        list4 = load_list("list4", offs4)
        step = new("step", PACK, F32)
        nc.scalar.dma_start(step[:], st.rearrange("(p t) o -> p (t o)", t=PACK))
        for t in (1, 2):
            nc.sync.dma_start(store[t][:], ca_rows[t])
        xt_sb = new("xt_sb", T, I32)
        nc.sync.dma_start(xt_sb[:], xt_words[0].rearrange("p c r -> p (c r)").bitcast(I32))
        list1 = load_list("list1", offs)
        load_scales(xt_plane, xt_scales)
        w_sb = new("w_sb", 2 * R, U8)
        nc.sync.dma_start(w_sb[:].bitcast(I32), w_words[0].bitcast(I32))
        load_scales(w_plane, w_scales)
        nc.sync.dma_start(store[3][:], ca_rows[3])
        xo_sb = new("xo_sb", T, I32)
        nc.sync.dma_start(xo_sb[:], xo_words[0].rearrange("p c r -> p (c r)").bitcast(I32))
        list2 = load_list("list2", offs2)
        load_scales(xo_plane, xo_scales)
        w0_sb = new("w0_sb", 2 * R, U8)
        nc.sync.dma_start(w0_sb[:].bitcast(I32), w0_words[0].bitcast(I32))
        load_scales(w0_plane, w0_scales)
        wb_sb = new("wb_sb", 2 * N, U8)
        nc.sync.dma_start(wb_sb[:].bitcast(I32), wb_words[0].bitcast(I32))
        load_scales(wb_plane, wb_scales)

        neg_step = new("neg_step", PACK, F32)
        nc.scalar.activation(neg_step[:], step[:], COPY, scale=-1.0)

        g_ps = {(h, u): ps.tile([P, 2 * P], F32, name="g_ps%d_%d" % (h, u), tag="bank%d" % (2 * u + h))
                for h in range(HALVES) for u in range(2)}
        g_sb = {}

        def difference(t):
            u, e = divmod(t, 2)
            for side, (lst, factor) in enumerate(((list3, step), (list4, neg_step))):
                codes = new("codes%d_%d" % (t, side), J, U8)
                nc.vector.tensor_copy(codes[:], store[t][:].indirect(lst[:]))
                vals = new("vals%d_%d" % (t, side), J, F32)
                nc.scalar.activation(vals[:], codes[:].bitcast(FP8), COPY, scale=factor[:, t:t + 1])
                for h in range(HALVES):
                    nc.tensor.matmul(g_ps[h, u][:, e * P:(e + 1) * P], lhsT=vals[:, h * P:(h + 1) * P], rhs=ident[:],
                                     is_transpose=True, start=(side == 0), stop=(side == 1))
            if e == 1:
                for h in range(HALVES):
                    g = new("g_sb%d_%d" % (h, u), 2 * P, F32)
                    nc.scalar.copy(g[:].rearrange("j (p e) -> j p e", e=2),
                                   g_ps[h, u][:].rearrange("j (e p) -> j p e", e=2))
                    g_sb[h, u] = g

        pieces = [(0, 0, R), (1, 0, R // 2), (1, R // 2, R)]
        a_ps = [ps.tile([P, hi - lo], F32, name="a_ps%d" % i, tag="bank%d" % (4 + i))
                for i, (h, lo, hi) in enumerate(pieces)]

        for t in range(3):
            difference(t)
        xt_g = new("xt_g", J, U32)
        nc.vector.tensor_copy(xt_g[:], xt_sb[:].bitcast(U32).indirect(list1[:]))
        xt_gs = new("xt_gs", J, U8)
        nc.vector.tensor_copy(xt_gs[:], xt_plane[:].indirect(list1[:]))
        for i, (h, lo, hi) in enumerate(pieces):
            cols = slice(h * P, (h + 1) * P)
            nc.tensor.matmul_mx(a_ps[i][:], lhsT=xt_g[:, cols].bitcast(E5M2X4), lhsT_scale=xt_gs[:, cols],
                                rhs=w_sb[:, 2 * lo:2 * hi].bitcast(E2M1X4), rhs_scale=w_plane[:, lo:hi],
                                start=True, stop=False)
        difference(3)
        for h in range(HALVES):
            part = list2[:, h * 8:(h + 1) * 8]
            xo_g = new("xo_g%d" % h, P, U32)
            nc.vector.tensor_copy(xo_g[:], xo_sb[:].bitcast(U32).indirect(part))
            xo_gs = new("xo_gs%d" % h, P, U8)
            nc.vector.tensor_copy(xo_gs[:], xo_plane[:].indirect(part))
            for i, (half, lo, hi) in enumerate(pieces):
                if half == h:
                    nc.tensor.matmul_mx(a_ps[i][:], lhsT=xo_g[:].bitcast(E4M3X4), lhsT_scale=xo_gs[:],
                                        rhs=w0_sb[:, 2 * lo:2 * hi].bitcast(E2M1X4), rhs_scale=w0_plane[:, lo:hi],
                                        start=False, stop=True)

        grouped = []
        for h in range(HALVES):
            turned = ps.tile([P, 2 * P], F32, name="turned%d" % h, tag="bank%d" % h)
            hid_t = [new("hid_t%d_%d" % (h, u), R // 2, BF16) for u in range(2)]
            for i, (half, lo, hi) in enumerate(pieces):
                if half == h:
                    for u in range(2):
                        cols = slice(lo // 2, hi // 2)
                        nc.vector.tensor_tensor(hid_t[u][:, cols].rearrange("j (p e) -> j p e", e=2),
                                                a_ps[i][:].rearrange("j (p u e) -> j u p e", u=2, e=2)[:, u],
                                                g_sb[h, u][:, cols].rearrange("j (p e) -> j p e", e=2), MULT)
            for u in range(2):
                nc.tensor.transpose(turned[:, u * P:(u + 1) * P], hid_t[u][:].bitcast(F32), ident[:])
            hid = new("hid%d" % h, R, BF16)
            nc.scalar.copy(hid[:].bitcast(F32).rearrange("p (j u) -> p j u", u=2),
                           turned[:].rearrange("p (u j) -> p j u", u=2))
            grouped.append(hid)

        for h in range(HALVES):
            hid_q = new("hid_q%d" % h, P, U32)
            hid_s = new("hid_s%d" % h, P, U8)
            nc.vector.quantize_mx(hid_q[:].bitcast(E4M3X4), hid_s[:], grouped[h][:])
            for b in range(N // P):
                o_ps = ps.tile([P, P], F32, name="o_ps%d_%d" % (h, b), tag="bank%d" % (2, 3, 7, 4)[2 * h + b])
                nc.tensor.matmul_mx(o_ps[:],
                                    lhsT=wb_sb[:, 2 * b * P:2 * (b + 1) * P].bitcast(E2M1X4),
                                    lhsT_scale=wb_plane[:, b * P:(b + 1) * P],
                                    rhs=hid_q[:].bitcast(E4M3X4), rhs_scale=hid_s[:], start=True, stop=True)
                o_sb = new("o_sb%d_%d" % (h, b), P, F32)
                dst = out[b * P:(b + 1) * P, h * P:(h + 1) * P]
                if b == 0:
                    nc.vector.tensor_copy(o_sb[:], o_ps[:])
                else:
                    nc.scalar.copy(o_sb[:], o_ps[:])
                queue = nc.scalar if h == 1 and b == 1 else nc.sync
                queue.dma_start(dst, o_sb[:])
